import numpy as np
import ml_dtypes


def mxq(x, axis, fmt="e4m3"):
    dtype, down = {"e4m3": (ml_dtypes.float8_e4m3fn, 7), "e5m2": (ml_dtypes.float8_e5m2, 14)}[fmt]
    v = np.moveaxis(np.asarray(x, np.float32).astype(ml_dtypes.bfloat16).astype(np.float64), axis, -1)
    blocks = v.reshape(v.shape[:-1] + (-1, 32))
    amax = np.abs(blocks).max(-1, keepdims=True)
    byte = np.maximum(np.where(amax > 0, np.frexp(amax)[1] - 1 + 127, 0) - down, 1)
    scale = np.exp2(byte - 127.0)
    codes = (blocks / scale).astype(np.float32).astype(dtype).astype(np.float64)
    return np.moveaxis((codes * scale).reshape(v.shape), -1, axis)


WIDE = False


def mx_kscale(k):
    if not WIDE:
        return np.ones(k)
    levels = np.array([10, -10, 5, -5, 0])
    if k % 512:
        return np.exp2(np.random.permutation(np.resize(levels, k // 32))).repeat(32)
    a = np.empty((k // 512, 16))
    for p in range(k // 512):
        a[p, :8] = np.random.permutation(np.resize(levels, 8))
        for g in range(8):
            far = levels[np.abs(levels - a[p, g]) >= 10]
            a[p, g + 8] = far[np.random.randint(len(far))]
    return np.exp2(a.ravel()).repeat(32)


BF16 = ml_dtypes.bfloat16


def bf(x):
    return np.asarray(x, np.float32).astype(BF16)


def f64(x):
    return np.asarray(x).astype(np.float64)

def planes(Y):
    n, m = Y.shape
    b = f64(bf(Y)).reshape(n // 32, 32, m)
    amax = np.abs(b).max(1)
    byte = np.clip(np.where(amax > 0, np.frexp(amax)[1] - 1 + 127 - 7, 1), 1, 254)
    codes = (b * np.exp2(127.0 - byte)[:, None, :]).reshape(n, m).astype(np.float32).astype(ml_dtypes.float8_e4m3fn).view(np.uint8)
    words = codes.reshape(n // 512, 128, 4, m).transpose(0, 1, 3, 2)
    return np.ascontiguousarray(words), np.ascontiguousarray(byte.astype(np.uint8).reshape(n // 512, 16, m))


N, M, D, E = 1024, 1024, 512, 1024

TAU = 0.8
LOSS_DIVISOR = 128.0


def softmax_rows(z):
    w = np.exp(z - z.max(axis=1, keepdims=True))
    return w / w.sum(axis=1, keepdims=True)


def setup_inputs():
    s, t = mx_kscale(D), mx_kscale(E)
    u = mx_kscale(M)
    fs = np.random.standard_normal((N, D)) / np.sqrt(D) * s
    ks = np.random.standard_normal((M, D)) / s[None, :] * u[:, None]
    a = (1.0 + 0.1 * np.random.standard_normal(M)) / u
    ft = np.random.standard_normal((N, E)) / np.sqrt(E) * t
    kt = np.random.standard_normal((M, E)) / t[None, :]
    return {"fs": bf(fs), "ks": bf(ks), "a": bf(a), "ft": bf(ft), "kt": bf(kt)}


def core(fs, ks, a, ft, kt):
    fs, ks, a, ft, kt = f64(fs), f64(ks), f64(a), f64(ft), f64(kt)
    m = ks.shape[0]
    zs = a[None, :] * (mxq(fs, 1, "e4m3") @ mxq(ks, 1, "e4m3").T) / TAU
    zt = (mxq(ft, 1, "e4m3") @ mxq(kt, 1, "e4m3").T) / TAU
    p = softmax_rows(zs)
    q = softmax_rows(zt)
    e = m * (p - q) * a[None, :]
    return (1.0 / (LOSS_DIVISOR * TAU)) * (mxq(e, 1, "e4m3") @ mxq(ks, 0, "e4m3"))


def reference(fs, ks, a, ft, kt):
    R_out = core(fs, ks, a, ft, kt)
    words, scales = planes(R_out)
    return R_out, words, scales

from contextlib import ExitStack

import concourse.mybir as mybir
from concourse.masks import make_identity

N, M, D, E = 1024, 1024, 512, 1024
FLOPS = 2 * N * M * (D + E + D)

P = 128
F32 = mybir.dt.float32
BF16 = mybir.dt.bfloat16
U32 = mybir.dt.uint32
I32 = mybir.dt.int32
U8 = mybir.dt.uint8
FP8X4 = mybir.dt.float8_e4m3fn_x4
ACT = mybir.ActivationFunctionType
ALU = mybir.AluOpType
AX = mybir.AxisListType


def tile_crossimagerelationalkdanchorgradient_x1_kernel(tc, fs, ks, a, ft, kt, out_0, out_1, out_2):
    nc = tc.nc
    with ExitStack() as ctx:
        raw = ctx.enter_context(tc.tile_pool(name="raw", bufs=1))
        keep = ctx.enter_context(tc.tile_pool(name="keep", bufs=1))
        grp = ctx.enter_context(tc.tile_pool(name="grp", bufs=2))
        work = ctx.enter_context(tc.tile_pool(name="work", bufs=3))
        psum = ctx.enter_context(tc.psum_pool(name="psum", bufs=1))
        ctx.enter_context(tc.manual_schedule())

        def bank(k):
            return psum.tile([P, 512], F32, name="b%d" % k, tag="b%d" % k)

        a_line = keep.tile([P, M], BF16, name="a_line")
        nc.vector.memset(a_line[:].bitcast(I32), 0)
        ones = keep.tile([P, P], BF16, name="ones")
        nc.vector.memset(ones[:], 1.0)
        nc.scalar.dma_start(out=a_line[0:1, :], in_=a.rearrange("(o m) -> o m", o=1))
        a_col16 = keep.tile([P, 2, 4], BF16, name="a_col16")
        nc.scalar.dma_start(out=a_col16[:], in_=a.rearrange("(g p t) -> p g t", p=P, t=4))

        def load(src, width, g, t0, nt, name):
            t = raw.tile([P, nt, width], BF16, name=name, tag=name)
            view = src[512 * g : 512 * (g + 1), :].rearrange("(p t) k -> p t k", t=4)
            nc.sync.dma_start(out=t[:], in_=view[:, t0 : t0 + nt, :])
            return t

        ks_raw, kt_raw, fs_raw, ft_raw = {}, {}, {}, {}
        def load_ks(g):
            ks_raw[g] = raw.tile([P, 4, D], BF16, name="ks%d" % g, tag="ks%d" % g)
            view = ks[512 * g : 512 * (g + 1), :].rearrange("(p t) k -> p t k", t=4)
            for h in (0, 1):
                nc.sync.dma_start(out=ks_raw[g][:, 2 * h : 2 * h + 2, :], in_=view[:, 2 * h : 2 * h + 2, :])

        load_ks(0)
        fs_raw[0, 0] = load(fs, D, 0, 0, 2, "fs00")
        load_ks(1)
        kt_raw[0, 0] = load(kt, E, 0, 0, 2, "kt00")
        kt_raw[0, 1] = load(kt, E, 0, 2, 2, "kt01")
        ft_raw[0, 0] = load(ft, E, 0, 0, 2, "ft00")
        kt_raw[1, 0] = load(kt, E, 1, 0, 2, "kt10")
        kt_raw[1, 1] = load(kt, E, 1, 2, 2, "kt11")
        fs_raw[0, 1] = load(fs, D, 0, 2, 2, "fs01")
        fs_raw[1, 0] = load(fs, D, 1, 0, 2, "fs10")
        fs_raw[1, 1] = load(fs, D, 1, 2, 2, "fs11")
        ft_raw[0, 1] = load(ft, E, 0, 2, 2, "ft01")
        ft_raw[1, 0] = load(ft, E, 1, 0, 2, "ft10")
        ft_raw[1, 1] = load(ft, E, 1, 2, 2, "ft11")

        ident = keep.tile([P, P], F32, name="ident")
        make_identity(nc, ident[:])
        warm = keep.tile([P, 1], F32, name="warm")
        nc.vector.memset(warm[:], 0.0)
        nc.scalar.activation(out=warm[:], in_=warm[:], func=ACT.Exp)

        a_col = keep.tile([P, 2, 4], F32, name="a_col")
        nc.gpsimd.tensor_scalar(out=a_col[:], in0=a_col16[:], scalar1=1024.0, scalar2=1.0, op0=ALU.mult, op1=ALU.mult)
        a_col125 = keep.tile([P, 2, 4], F32, name="a_col125")
        nc.gpsimd.tensor_scalar(out=a_col125[:], in0=a_col16[:], scalar1=1.25, scalar2=1.0, op0=ALU.mult, op1=ALU.mult)
        a_row = keep.tile([P, M], F32, name="a_row")
        for g in (0, 1):
            b = bank(g)
            nc.tensor.matmul(b[:], lhsT=ones[:], rhs=a_line[:, 512 * g : 512 * (g + 1)], start=True, stop=True)
            nc.scalar.activation(
                out=a_row[:, 512 * g : 512 * (g + 1)].rearrange("p (t m) -> p t m", t=4),
                in_=b[:].rearrange("p (m t) -> p t m", t=4),
                func=ACT.Copy, scale=1.25,
            )

        def copy(eng, out, in_):
            if eng == "s":
                nc.scalar.copy(out=out, in_=in_)
            else:
                nc.vector.tensor_copy(out=out, in_=in_)

        ks_grp, ks_codes, ks_sc = {}, {}, {}
        kt_grp, kt_codes, kt_sc = {}, {}, {}
        fs_grp, fs_codes, fs_sc = {}, {}, {}
        ft_grp, ft_codes, ft_sc = {}, {}, {}
        for g in (0, 1):
            ks_codes[g] = keep.tile([P, 512], U32, name="ks_codes%d" % g, align_bytes=64)
            ks_sc[g] = keep.tile([P, 512], U8, name="ks_sc%d" % g, align_bytes=64)
            kt_codes[g] = keep.tile([P, 2, 512], U32, name="kt_codes%d" % g, align_bytes=64)
            kt_sc[g] = keep.tile([P, 2, 512], U8, name="kt_sc%d" % g, align_bytes=64)
            fs_codes[g] = keep.tile([P, 512], U32, name="fs_codes%d" % g, align_bytes=64)
            fs_sc[g] = keep.tile([P, 512], U8, name="fs_sc%d" % g, align_bytes=64)
            ks_grp[g] = grp.tile([P, 512, 4], BF16, name="ks_grp", tag="ks_grp", align_bytes=64)
            kt_grp[g] = grp.tile([P, 2, 512, 4], BF16, name="kt_grp", tag="kt_grp", align_bytes=64)
        for j in range(8):
            ft_codes[j] = keep.tile([P, 2, P], U32, name="ft_codes%d" % j, align_bytes=64)
            ft_sc[j] = keep.tile([P, 2, P], U8, name="ft_sc%d" % j, align_bytes=64)

        def quant(codes, scales, values):
            nc.vector.quantize_mx(out=codes.bitcast(FP8X4), scales=scales, in_=values)

        def turn_512(src, b):
            words = src.bitcast(F32)
            for blk in (0, 1):
                for u in (0, 1):
                    c = 256 * blk + 128 * u
                    nc.tensor.transpose(b[:, c : c + 128], words[:, blk, u:256:2], ident[:])

        def evac_512(eng, b, grouped):
            copy(eng, grouped.bitcast(F32).rearrange("p (b r u) -> p b r u", b=2, u=2),
                 b[:].rearrange("p (b u r) -> p b r u", b=2, u=2))

        def turn_1024(src, blk, b):
            words = src[:].bitcast(F32)
            for q in (0, 1):
                for u in (0, 1):
                    c = 256 * q + 128 * u
                    nc.tensor.transpose(b[:, c : c + 128], words[:, blk, 256 * q + u : 256 * (q + 1) : 2], ident[:])

        def evac_1024(eng, b, grouped):
            copy(eng, grouped.rearrange("p q r t -> p q (r t)").bitcast(F32).rearrange("p q (r u) -> p q r u", u=2),
                 b[:].rearrange("p (q u r) -> p q r u", q=2, u=2))

        rot = [4, 5, 6, 7, 2, 3]
        state = {"n": 0}

        def next_bank():
            k = rot[state["n"] % len(rot)]
            state["n"] = state["n"] + 1
            return bank(k)

        tb = {}

        def tp_ks(g, h):
            tb["ks", g, h] = next_bank()
            turn_512(ks_raw[g][:, 2 * h : 2 * h + 2, :], tb["ks", g, h])

        def ev_ks(g, h, eng):
            evac_512(eng, tb["ks", g, h], ks_grp[g][:, 256 * h : 256 * (h + 1), :].rearrange("p r t -> p (r t)"))

        def ks_quant(g):
            quant(ks_codes[g][:], ks_sc[g][:], ks_grp[g][:].rearrange("p r t -> p (r t)"))

        def tp_fs(g, h):
            tb["fs", g, h] = next_bank()
            fs_grp[g, h] = grp.tile([P, 256, 4], BF16, name="fs_grp", tag="fs_grp", align_bytes=64)
            turn_512(fs_raw[g, h][:], tb["fs", g, h])

        def ev_fs(g, h, eng):
            evac_512(eng, tb["fs", g, h], fs_grp[g, h][:].rearrange("p r t -> p (r t)"))

        def fs_quant(g, h):
            sl = slice(256 * h, 256 * (h + 1))
            quant(fs_codes[g][:, sl], fs_sc[g][:, sl], fs_grp[g, h][:].rearrange("p r t -> p (r t)"))

        def tp_kt(g, t):
            tb["kt", g, t] = next_bank()
            turn_1024(kt_raw[g, t // 2], t % 2, tb["kt", g, t])

        def ev_kt(g, t, eng):
            evac_1024(eng, tb["kt", g, t], kt_grp[g][:, :, 128 * t : 128 * (t + 1), :])

        def kt_quant(g, q):
            quant(kt_codes[g][:, q, :], kt_sc[g][:, q, :], kt_grp[g][:, q, :, :].rearrange("p r t -> p (r t)"))

        def tp_ft(j):
            tb["ft", j] = next_bank()
            g, t = j // 4, j % 4
            ft_grp[j] = grp.tile([P, 2, P, 4], BF16, name="ft_grp", tag="ft_grp", align_bytes=64)
            turn_1024(ft_raw[g, t // 2], t % 2, tb["ft", j])

        def ev_ft(j, eng):
            evac_1024(eng, tb["ft", j], ft_grp[j][:])

        def ft_quant(j):
            quant(ft_codes[j][:].rearrange("p q r -> p (q r)"), ft_sc[j][:].rearrange("p q r -> p (q r)"),
                  ft_grp[j][:].rearrange("p q r t -> p (q r t)"))

        k0_grp, k0_codes, k0_sc = {}, {}, {}

        def k0_copy(g):
            k0_grp[g] = keep.tile([P, D, 4], BF16, name="k0_grp%d" % g, align_bytes=64)
            nc.gpsimd.tensor_scalar(
                out=k0_grp[g][:], in0=ks_raw[g][:].rearrange("p t d -> p d t"),
                scalar1=1.0, scalar2=1.0, op0=ALU.mult, op1=ALU.mult,
            )

        def k0_quant(g):
            k0_codes[g] = keep.tile([P, D], U32, name="k0_codes%d" % g, align_bytes=64)
            k0_sc[g] = keep.tile([P, D], U8, name="k0_sc%d" % g, align_bytes=64)
            quant(k0_codes[g][:], k0_sc[g][:], k0_grp[g][:].rearrange("p d t -> p (d t)"))

        zs, zt, x, p, q, vst, sst, rec, eb, ec, es, et = {}, {}, {}, {}, {}, {}, {}, {}, {}, {}, {}, {}
        of = {}

        def z_s(j):
            g, t = j // 4, j % 4
            lo = 128 * t
            for h in (0, 1):
                zs[j, h] = bank(h)
                nc.tensor.matmul_mx(
                    zs[j, h][:], lhsT=fs_codes[g][:, lo : lo + 128].bitcast(FP8X4), lhsT_scale=fs_sc[g][:, lo : lo + 128],
                    rhs=ks_codes[h][:].bitcast(FP8X4), rhs_scale=ks_sc[h][:], start=True, stop=True,
                )

        xt = {}

        def zt_mm(b):
            if b == 0:
                xt[0] = keep.tile([P, 8, 512], F32, name="xt")
            g, t = b // 4, b % 4
            tb["zt", b] = next_bank()
            nc.tensor.matmul_mx(
                tb["zt", b][:], lhsT=ks_codes[g][:, 128 * t : 128 * (t + 1)].bitcast(FP8X4), lhsT_scale=ks_sc[g][:, 128 * t : 128 * (t + 1)],
                rhs=fs_codes[1][:].bitcast(FP8X4), rhs_scale=fs_sc[1][:], start=True, stop=True,
            )

        def zt_ev(b, eng):
            g, t = b // 4, b % 4
            o = tb["zt", b]
            if eng == "s":
                nc.scalar.activation(out=xt[0][:, b, :], in_=o[:], func=ACT.Copy, scale=a_col125[:, g, t : t + 1])
            else:
                nc.vector.tensor_scalar(out=xt[0][:, b, :], in0=o[:], scalar1=a_col125[:, g, t : t + 1], scalar2=1.0, op0=ALU.mult, op1=ALU.mult)

        def turn_x(j):
            for h in (0, 1):
                zs[j, h] = bank(h)
                for t in range(4):
                    nc.tensor.transpose(zs[j, h][:, 128 * t : 128 * (t + 1)], xt[0][:, 4 * h + t, 128 * (j - 4) : 128 * (j - 3)], ident[:])

        def z_t(j):
            for h in (0, 1):
                zt[j, h] = bank(2 + h)
                for c in (0, 1):
                    nc.tensor.matmul_mx(
                        zt[j, h][:], lhsT=ft_codes[j][:, c, :].bitcast(FP8X4), lhsT_scale=ft_sc[j][:, c, :],
                        rhs=kt_codes[h][:, c, :].bitcast(FP8X4), rhs_scale=kt_sc[h][:, c, :], start=(c == 0), stop=(c == 1),
                    )

        def v_x(j):
            vst[j] = work.tile([P, 8], F32, name="vst", tag="vst")
            sst[j] = work.tile([P, 8], F32, name="sst", tag="sst")
            if j >= 4:
                return
            x[j] = work.tile([P, M], F32, name="x", tag="x")
            for h in (0, 1):
                sl = slice(512 * h, 512 * (h + 1))
                nc.vector.tensor_tensor(out=x[j][:, sl], in0=zs[j, h][:], in1=a_row[:, sl], op=ALU.mult)

        def v_maxx(j):
            if j >= 4:
                for h in (0, 1):
                    nc.vector.tensor_reduce(out=vst[j][:, 4 + h : 5 + h], in_=zs[j, h][:], axis=AX.X, op=ALU.max)
                return
            nc.vector.tensor_reduce(out=vst[j][:, 0:1], in_=x[j][:], axis=AX.X, op=ALU.max, negate=True)

        def v_maxt(j):
            for h in (0, 1):
                nc.vector.tensor_reduce(out=vst[j][:, 1 + h : 2 + h], in_=zt[j, h][:], axis=AX.X, op=ALU.max)

        def v_combx(j):
            if j >= 4:
                nc.vector.tensor_scalar(out=vst[j][:, 0:1], in0=vst[j][:, 4:5], scalar1=vst[j][:, 5:6], scalar2=-1.0, op0=ALU.max, op1=ALU.mult)

        def v_comb(j):
            nc.vector.tensor_scalar(out=vst[j][:, 3:4], in0=vst[j][:, 1:2], scalar1=vst[j][:, 2:3], scalar2=-1.25, op0=ALU.max, op1=ALU.mult)

        def s_x(j):
            p[j] = work.tile([P, M], F32, name="p", tag="p")
            if j >= 4:
                for h in (0, 1):
                    nc.scalar.activation(out=p[j][:, 512 * h : 512 * (h + 1)], in_=zs[j, h][:], func=ACT.Exp, bias=vst[j][:, 0:1], scale=1.0,
                                         accum_out=sst[j][:, 4 + h : 5 + h])
                nc.scalar.activation(out=sst[j][:, 0:1], in_=sst[j][:, 4:5], func=ACT.Identity, bias=sst[j][:, 5:6], scale=1.0)
                return
            nc.scalar.activation(out=p[j][:], in_=x[j][:], func=ACT.Exp, bias=vst[j][:, 0:1], scale=1.0, accum_out=sst[j][:, 0:1])

        def s_t(j):
            q[j] = work.tile([P, M], F32, name="q", tag="q")
            for h in (0, 1):
                nc.scalar.activation(out=q[j][:, 512 * h : 512 * (h + 1)], in_=zt[j, h][:], func=ACT.Exp, bias=vst[j][:, 3:4], scale=1.25,
                                     accum_out=sst[j][:, 2 + h : 3 + h])
            nc.scalar.activation(out=sst[j][:, 1:2], in_=sst[j][:, 2:3], func=ACT.Identity, bias=sst[j][:, 3:4], scale=1.0)

        def v_rec(j):
            rec[j] = work.tile([P, 2], F32, name="rec", tag="rec")
            nc.vector.reciprocal(out=rec[j][:], in_=sst[j][:, 0:2])

        def g_scale(j):
            nc.gpsimd.tensor_scalar(out=q[j][:], in0=q[j][:], scalar1=rec[j][:, 1:2], scalar2=-1.0, op0=ALU.mult, op1=ALU.mult)
            nc.gpsimd.tensor_scalar(out=p[j][:], in0=p[j][:], scalar1=rec[j][:, 0:1], scalar2=1.0, op0=ALU.mult, op1=ALU.mult)

        def fast_scale(j, h):
            sl = slice(512 * h, 512 * (h + 1))
            nc.vector.tensor_scalar(out=q[j][:, sl], in0=q[j][:, sl], scalar1=rec[j][:, 1:2], scalar2=-1.0, op0=ALU.mult, op1=ALU.mult)
            nc.scalar.activation(out=p[j][:, sl], in_=p[j][:, sl], func=ACT.Copy, scale=rec[j][:, 0:1])

        def turn_e(j, gs=(0, 1)):
            for g in gs:
                et[j, g] = bank(4 + g)
                for t in range(4):
                    sl = slice(512 * g + 128 * t, 512 * g + 128 * (t + 1))
                    o = et[j, g][:, 128 * t : 128 * (t + 1)]
                    nc.tensor.matmul(o, lhsT=p[j][:, sl], rhs=ident[:], is_transpose=True, start=True, stop=False)
                    nc.tensor.matmul(o, lhsT=q[j][:, sl], rhs=ident[:], is_transpose=True, start=False, stop=True)

        def v_e(j, gs=(0, 1)):
            if 0 in gs:
                eb[j] = work.tile([P, 2, P, 4], BF16, name="eb", tag="eb", align_bytes=64)
            for g in gs:
                nc.vector.tensor_tensor(
                    out=eb[j][:, g, :, :], in0=et[j, g][:].rearrange("p (t n) -> p n t", t=4),
                    in1=a_col[:, g, :].unsqueeze(1).to_broadcast([P, P, 4]), op=ALU.mult,
                )

        def v_eq(j):
            ec[j] = work.tile([P, 2, P], U32, name="ec", tag="ec", align_bytes=64)
            es[j] = work.tile([P, 2, P], U8, name="es", tag="es", align_bytes=64)
            quant(ec[j][:].rearrange("p g n -> p (g n)"), es[j][:].rearrange("p g n -> p (g n)"), eb[j][:].rearrange("p g n t -> p (g n t)"))

        ob = {}

        def o_mm(j):
            ob[j] = bank(6 + j % 2)
            for g in (0, 1):
                nc.tensor.matmul_mx(
                    ob[j][:], lhsT=ec[j][:, g, :].bitcast(FP8X4), lhsT_scale=es[j][:, g, :],
                    rhs=k0_codes[g][:].bitcast(FP8X4), rhs_scale=k0_sc[g][:], start=(g == 0), stop=(g == 1),
                )

        def s_out(j):
            g, t = j // 4, j % 4
            if t == 0:
                of[g] = keep.tile([P, 4, D], F32, name="of%d" % g)
            nc.scalar.activation(out=of[g][:, t, :], in_=ob[j][:], func=ACT.Copy, scale=5.0 / 512.0)
            view = out_0[512 * g : 512 * (g + 1), :].rearrange("(p t) d -> p t d", t=4)
            nc.sync.dma_start(out=view[:, t, :], in_=of[g][:, t, :])

        pb, pc, ps = {}, {}, {}

        def planes_tiles(g):
            pb[g] = keep.tile([P, D, 4], BF16, name="pb%d" % g, align_bytes=64)
            pc[g] = keep.tile([P, D], U32, name="pc%d" % g, align_bytes=64)
            ps[g] = keep.tile([P, D], U8, name="ps%d" % g, align_bytes=64)

        def planes_quant(g, lo, hi):
            quant(pc[g][:, lo:hi], ps[g][:, lo:hi], pb[g][:, lo:hi, :].rearrange("p d t -> p (d t)"))

        def planes_store(g):
            nc.sync.dma_start(out=out_1[g].rearrange("p m t -> p (m t)").bitcast(I32), in_=pc[g][:].bitcast(I32))
            for k in range(4):
                nc.sync.dma_start(out=out_2[g, 4 * k : 4 * k + 4, :].bitcast(I32), in_=ps[g][32 * k : 32 * k + 4, :].bitcast(I32))

        tp_ks(0, 0)
        tp_ks(0, 1)
        tp_fs(0, 0)
        ev_ks(0, 0, "s")
        ev_ks(0, 1, "v")
        ks_quant(0)
        ev_fs(0, 0, "s")
        fs_quant(0, 0)
        tp_ks(1, 0)
        tp_ks(1, 1)
        ev_ks(1, 0, "v")
        ev_ks(1, 1, "s")
        ks_quant(1)
        k0_copy(0)
        k0_copy(1)
        tp_kt(0, 0)
        tp_kt(0, 1)
        z_s(0)
        ev_kt(0, 0, "s")
        ev_kt(0, 1, "s")
        v_x(0)
        tp_kt(0, 2)
        tp_kt(0, 3)
        v_maxx(0)
        z_s(1)
        ev_kt(0, 2, "s")
        ev_kt(0, 3, "s")
        tp_ft(0)
        tp_kt(1, 0)
        tp_kt(1, 1)
        s_x(0)
        v_x(1)
        kt_quant(0, 0)
        kt_quant(0, 1)
        v_maxx(1)
        ev_ft(0, "s")
        ev_kt(1, 0, "s")
        ev_kt(1, 1, "s")
        tp_kt(1, 2)
        tp_kt(1, 3)
        tp_fs(0, 1)
        ft_quant(0)
        k0_quant(0)
        k0_quant(1)
        ev_kt(1, 2, "s")
        ev_kt(1, 3, "v")
        kt_quant(1, 0)
        kt_quant(1, 1)
        tp_fs(1, 0)
        tp_fs(1, 1)
        s_x(1)
        ev_fs(0, 1, "s")
        fs_quant(0, 1)
        z_t(0)
        ev_fs(1, 0, "s")
        ev_fs(1, 1, "s")
        rot[:] = [6, 7]
        tp_ft(1)
        ev_ft(1, "s")
        z_s(2)

        for i in range(9):
            if 3 <= i:
                s_out(i - 3)
            if 1 <= i < 8:
                v_rec(i - 1)
                g_scale(i - 1)
            if i == 6:
                planes_tiles(0)
                nc.gpsimd.tensor_scalar(out=pb[0][:], in0=of[0][:].rearrange("p t d -> p d t"), scalar1=1.0, scalar2=1.0, op0=ALU.mult, op1=ALU.mult)
            if i == 0:
                fs_quant(1, 0)
                fs_quant(1, 1)
                ft_quant(1)
            if i + 2 < 8:
                tp_ft(i + 2)
                ev_ft(i + 2, "s")
            if i < 8:
                v_maxt(i)
            if 2 <= i <= 8:
                v_e(i - 2)
            if i < 8:
                v_comb(i)
            if i in (0, 1):
                for b in range(4):
                    zt_mm(4 * i + b)
                    zt_ev(4 * i + b, "s")
                    if b == 1:
                        s_t(i)
            elif i < 8:
                s_t(i)
            if 1 <= i and i + 1 < 8:
                v_x(i + 1)
                v_maxx(i + 1)
            if i + 2 < 8:
                ft_quant(i + 2)
            if 1 <= i and i + 1 < 8:
                v_combx(i + 1)
                s_x(i + 1)
            if 1 <= i < 8:
                turn_e(i - 1)
            if i + 1 < 8:
                z_t(i + 1)
            if 2 <= i <= 8:
                v_eq(i - 2)
                o_mm(i - 2)
            if i >= 1 and i + 2 < 8:
                if i + 2 < 4:
                    z_s(i + 2)
                else:
                    turn_x(i + 2)

        v_rec(7)
        fast_scale(7, 0)
        fast_scale(7, 1)
        turn_e(7, (0,))
        turn_e(7, (1,))
        v_e(7, (0,))
        v_e(7, (1,))
        v_eq(7)
        o_mm(7)
        s_out(6)
        planes_quant(0, 0, 512)
        planes_store(0)
        s_out(7)
        planes_tiles(1)
        nc.vector.tensor_copy(out=pb[1][:, 0:256, :], in_=of[1][:, :, 0:256].rearrange("p t d -> p d t"))
        nc.scalar.copy(out=pb[1][:, 256:512, :], in_=of[1][:, :, 256:512].rearrange("p t d -> p d t"))
        planes_quant(1, 0, 256)
        planes_quant(1, 256, 512)
        planes_store(1)
